import numpy as np
import ml_dtypes


def mxq(x, axis, fmt="e4m3"):
    dtype, down = {"e4m3": (ml_dtypes.float8_e4m3fn, 7), "e5m2": (ml_dtypes.float8_e5m2, 14)}[fmt]
    v = np.moveaxis(np.asarray(x, np.float32).astype(ml_dtypes.bfloat16).astype(np.float64), axis, -1)
    blocks = v.reshape(v.shape[:-1] + (-1, 32))
    amax = np.abs(blocks).max(-1, keepdims=True)
    byte = np.maximum(np.where(amax > 0, np.frexp(amax)[1] - 1 + 127, 0) - down, 1)
    scale = np.exp2(byte - 127.0)
    codes = (blocks / scale).astype(np.float32).astype(dtype).astype(np.float64)
    return np.moveaxis((codes * scale).reshape(v.shape), -1, axis)


WIDE = False


def mx_kscale(k):
    if not WIDE:
        return np.ones(k)
    levels = np.array([10, -10, 5, -5, 0])
    if k % 512:
        return np.exp2(np.random.permutation(np.resize(levels, k // 32))).repeat(32)
    a = np.empty((k // 512, 16))
    for p in range(k // 512):
        a[p, :8] = np.random.permutation(np.resize(levels, 8))
        for g in range(8):
            far = levels[np.abs(levels - a[p, g]) >= 10]
            a[p, g + 8] = far[np.random.randint(len(far))]
    return np.exp2(a.ravel()).repeat(32)


BF16 = ml_dtypes.bfloat16


def bf(x):
    return np.asarray(x, np.float32).astype(BF16)


def f64(x):
    return np.asarray(x).astype(np.float64)


H, N, E, C, T, EV = 4, 512, 512, 2, 512, 512
M = C * T


def per_source_softmax(s):
    top = np.max(s, axis=-1, keepdims=True)
    w = np.exp(s - top)
    return w / np.sum(w, axis=-1, keepdims=True)


def draw0():
    s, t = mx_kscale(E), mx_kscale(M)
    return {"q": bf(np.random.standard_normal((H, N, E)) * s),
            "k": bf(1.5 * np.random.standard_normal((H, M, E)) / s),
            "v": bf(0.3 * np.random.standard_normal((H, M, EV)) / t[:, None]),
            "g": bf(0.25 * np.sqrt(M) * np.random.standard_normal(M) * t),
            "lam": bf(np.random.uniform(0.3, 1.5, (N, C)))}


def core(q, k, v, g, lam):
    q, k, v, g, lam = f64(q), f64(k), f64(v), f64(g), f64(lam)
    heads, n_pos, width = q.shape
    n_tok = k.shape[1]
    n_src = lam.shape[1]
    per_src = n_tok // n_src

    s = (mxq(q, 2, "e4m3") @ mxq(k, 2, "e4m3").transpose(0, 2, 1)) / np.sqrt(width)

    p = per_source_softmax(s.reshape(heads, n_pos, n_src, per_src))

    r = p * lam[None, :, :, None]

    a = r.reshape(heads, n_pos, n_tok) * g[None, None, :]

    return mxq(a, 2, "e4m3") @ mxq(v, 1, "e4m3")


def e4m3fn_bytes(y):
    return np.clip(np.asarray(y, np.float64), -448.0, 448.0).astype(np.float32).astype(ml_dtypes.float8_e4m3fn).view(np.uint8)


def e4m3fn_values(b):
    return np.asarray(b, np.uint8).view(ml_dtypes.float8_e4m3fn).astype(np.float64)


def setup_inputs():
    d = draw0()
    x0 = np.asarray(d['v']).astype(np.float64)
    s = (np.max(np.abs(x0), axis=(0, 2), keepdims=True) / 448.0).astype(np.float32)
    out = {}
    for k, v in d.items():
        if k == 'v':
            out['v_bytes'] = e4m3fn_bytes(x0 / s.astype(np.float64))
            out['v_scale'] = s
        else:
            out[k] = v
    return out


def reference(q, k, v_bytes, v_scale, g, lam):
    return core(q, k, e4m3fn_values(v_bytes) * v_scale.astype(np.float64), g, lam)

@@ -1,0 +1,344 @@
+import math
+from contextlib import ExitStack
+
+import concourse.mybir as mybir
+from concourse.masks import make_identity
+
+HEADS, N_POS, WIDTH, N_SRC, PER_SRC, V_WIDTH = 4, 512, 512, 2, 512, 512
+FLOPS = 2 * HEADS * N_POS * N_SRC * PER_SRC * (WIDTH + V_WIDTH)
+
+F32 = mybir.dt.float32
+BF16 = mybir.dt.bfloat16
+U32 = mybir.dt.uint32
+U8 = mybir.dt.uint8
+E4M3 = mybir.dt.float8_e4m3fn
+FP8X4 = mybir.dt.float8_e4m3fn_x4
+ACT = mybir.ActivationFunctionType
+ALU = mybir.AluOpType
+AX = mybir.AxisListType
+
+P = 128
+PACK = 4
+ROW_TILES = N_POS // P
+UNITS = HEADS * ROW_TILES
+SPLIT = 256
+SCALE = 1.0 / math.sqrt(WIDTH)
+
+
+def tile_ipadapterregionaldecoupledcrossattention_kernel(tc, q, k, v_bytes, v_scale, g, lam, out):
+    nc = tc.nc
+    with ExitStack() as ctx:
+        const = ctx.enter_context(tc.tile_pool(name="const", bufs=1))
+        raw = ctx.enter_context(tc.tile_pool(name="raw", bufs=1))
+        work = ctx.enter_context(tc.tile_pool(name="work", bufs=3))
+        small = ctx.enter_context(tc.tile_pool(name="small", bufs=4))
+        codes = ctx.enter_context(tc.tile_pool(name="codes", bufs=2))
+        psum = ctx.enter_context(tc.psum_pool(name="psum", bufs=1))
+        ctx.enter_context(tc.manual_schedule())
+
+        def bank(tag):
+            t = psum.tile([P, 512], F32, tag=tag, name=tag)
+            return t
+
+        q_raw, k_raw, v_raw = {}, {}, {}
+        for h in range(HEADS):
+            q_raw[h] = raw.tile([P, ROW_TILES, WIDTH], BF16, name="q_raw%d" % h)
+            for c in range(N_SRC):
+                k_raw[h, c] = raw.tile([P, PACK, WIDTH], BF16, name="k_raw%d_%d" % (h, c))
+            v_raw[h] = raw.tile([P, N_SRC, PACK, V_WIDTH], U8, name="v_raw%d" % h)
+
+        def load_q(h, r0, r1):
+            nc.sync.dma_start(out=q_raw[h][:, r0:r1, :], in_=q[h].rearrange("(p r) e -> p r e", r=ROW_TILES)[:, r0:r1, :])
+
+        def load_k(h, c, t0, t1):
+            nc.sync.dma_start(
+                out=k_raw[h, c][:, t0:t1, :],
+                in_=k[h, c * PER_SRC : (c + 1) * PER_SRC, :].rearrange("(p t) e -> p t e", t=PACK)[:, t0:t1, :],
+            )
+
+        def load_v(h):
+            nc.sync.dma_start(out=v_raw[h][:], in_=v_bytes[h].rearrange("(c p t) n -> p c t n", p=P, t=PACK))
+
+        load_k(0, 0, 0, 2)
+        load_k(0, 0, 2, 4)
+        load_q(0, 0, 2)
+        load_k(0, 1, 0, 2)
+        load_k(0, 1, 2, 4)
+        load_q(0, 2, 4)
+        load_k(1, 0, 0, 4)
+        load_v(0)
+        for h in range(1, HEADS):
+            if h > 1:
+                load_k(h, 0, 0, 4)
+            load_k(h, 1, 0, 4)
+            load_q(h, 0, 4)
+            load_v(h)
+
+        v_sc = const.tile([P, N_SRC * PACK], F32)
+        g_bf = const.tile([P, N_SRC * PACK], BF16)
+        lam_bf = const.tile([P, ROW_TILES * N_SRC], BF16)
+        nc.scalar.dma_start(out=v_sc[:].rearrange("p (c t) -> p c t", t=PACK), in_=v_scale.rearrange("o (c p t) u -> p (o c) (t u)", p=P, t=PACK))
+        nc.scalar.dma_start(out=g_bf[:].rearrange("p (c t) -> p c t", t=PACK), in_=g.rearrange("(c p t) -> p c t", p=P, t=PACK))
+        nc.scalar.dma_start(out=lam_bf[:], in_=lam.rearrange("(p r) c -> p (r c)", r=ROW_TILES))
+
+        warm = const.tile([P, 1], F32)
+        nc.gpsimd.memset(warm[:], 0.0)
+        ident = const.tile([P, P], F32)
+        make_identity(nc, ident[:])
+        warm_out = const.tile([P, 1], F32)
+        nc.scalar.activation(out=warm_out[:], in_=warm[:], func=ACT.Exp)
+        g_f = const.tile([P, N_SRC * PACK], F32)
+        nc.gpsimd.tensor_copy(out=g_f[:], in_=g_bf[:])
+        lam_f = const.tile([P, ROW_TILES * N_SRC], F32)
+        nc.gpsimd.tensor_copy(out=lam_f[:], in_=lam_bf[:])
+
+        q_codes, q_scales, k_codes, k_scales, v_codes, v_scales = {}, {}, {}, {}, {}, {}
+        grouped = {}
+
+        def job_copy(job, tag, engine):
+            kind, h, c, half = job
+            src = q_raw[h] if kind == "q" else k_raw[h, c]
+            b = bank(tag)
+            view = b[:].rearrange("p (s u r) -> p s u r", s=2, u=2)
+            for s in range(2):
+                words = src[:, 2 * half + s, :].bitcast(F32)
+                for u in range(2):
+                    nc.tensor.transpose(view[:, s, u, :], words[:, u : WIDTH // 2 : 2], ident[:])
+            xg = work.tile([P, 1024], BF16, tag="xg", name="xg", align_bytes=64)
+            grouped[job] = xg
+            dst = xg[:].bitcast(F32).rearrange("p (s r u) -> p s r u", s=2, u=2)
+            srcv = view.rearrange("p s u r -> p s r u")
+            if engine == "S":
+                nc.scalar.copy(out=dst, in_=srcv)
+            else:
+                nc.vector.tensor_copy(out=dst, in_=srcv)
+
+        def job_quant(job):
+            kind, h, c, half = job
+            if kind == "q":
+                if half == 0:
+                    q_codes[h] = codes.tile([P, N_POS], U32, tag="q_codes", name="q_codes", align_bytes=64)
+                    q_scales[h] = codes.tile([P, N_POS], U8, tag="q_scales", name="q_scales", align_bytes=64)
+                cc, ss = q_codes[h], q_scales[h]
+            else:
+                if half == 0:
+                    k_codes[h, c] = codes.tile([P, PER_SRC], U32, tag="k_codes%d" % c, name="k_codes", align_bytes=64)
+                    k_scales[h, c] = codes.tile([P, PER_SRC], U8, tag="k_scales%d" % c, name="k_scales", align_bytes=64)
+                cc, ss = k_codes[h, c], k_scales[h, c]
+            cols = slice(256 * half, 256 * (half + 1))
+            nc.vector.quantize_mx(out=cc[:, cols].bitcast(FP8X4), scales=ss[:, cols], in_=grouped[job][:])
+
+        wide, inter = {}, {}
+
+        def v_widen(h, c, t, engine="S"):
+            if t == 0:
+                wide[h, c] = work.tile([P, PACK, V_WIDTH], BF16, tag="wide", name="wide")
+            dst, src, sc = wide[h, c][:, t, :], v_raw[h][:, c, t, :].bitcast(E4M3), v_sc[:, PACK * c + t : PACK * c + t + 1]
+            if engine == "S":
+                nc.scalar.activation(out=dst, in_=src, func=ACT.Copy, scale=sc)
+            else:
+                nc.vector.tensor_scalar(out=dst, in0=src, scalar1=sc, scalar2=None, op0=ALU.mult)
+
+        def v_inter(h, c, lo, hi, engine):
+            if lo == 0:
+                inter[h, c] = work.tile([P, V_WIDTH, PACK], BF16, tag="inter", name="inter", align_bytes=64)
+            dst, src = inter[h, c][:, lo:hi, :], wide[h, c][:, :, lo:hi].rearrange("p t n -> p n t")
+            if engine == "V":
+                nc.vector.tensor_copy(out=dst, in_=src)
+            else:
+                nc.gpsimd.tensor_scalar(out=dst, in0=src, scalar1=1.0, scalar2=0.0, op0=ALU.mult, op1=ALU.add)
+
+        def v_quant(h, c):
+            v_codes[h, c] = codes.tile([P, V_WIDTH], U32, tag="v_codes%d" % c, name="v_codes", align_bytes=64)
+            v_scales[h, c] = codes.tile([P, V_WIDTH], U8, tag="v_scales%d" % c, name="v_scales", align_bytes=64)
+            nc.vector.quantize_mx(
+                out=v_codes[h, c][:].bitcast(FP8X4), scales=v_scales[h, c][:], in_=inter[h, c][:].rearrange("p n t -> p (n t)")
+            )
+
+        s_bank, e_tile, p_tile, t_bank, a_tile, a_codes, a_scales, top, ssum, rinv, bias, o_bank = {}, {}, {}, {}, {}, {}, {}, {}, {}, {}, {}, {}
+
+        def mm_scores(i):
+            h, r = divmod(i, ROW_TILES)
+            cols = slice(P * r, P * (r + 1))
+            for c in range(N_SRC):
+                s_bank[i, c] = bank("s%d" % (2 * (i % 2) + c))
+                nc.tensor.matmul_mx(
+                    out=s_bank[i, c][:],
+                    lhsT=q_codes[h][:, cols].bitcast(FP8X4),
+                    lhsT_scale=q_scales[h][:, cols],
+                    rhs=k_codes[h, c][:].bitcast(FP8X4),
+                    rhs_scale=k_scales[h, c][:],
+                    start=True,
+                    stop=True,
+                )
+
+        def row_max(i, c):
+            if c == 0:
+                top[i] = small.tile([P, N_SRC], F32, tag="top", name="top")
+            nc.vector.reduce_max(out=top[i][:, c : c + 1], in_=s_bank[i, c][:], axis=AX.X)
+
+        def neg_scale(i):
+            bias[i] = small.tile([P, N_SRC], F32, tag="bias", name="bias")
+            nc.vector.tensor_scalar(out=bias[i][:], in0=top[i][:], scalar1=-SCALE, scalar2=None, op0=ALU.mult)
+
+        def exps(i):
+            ssum[i] = small.tile([P, N_SRC], F32, tag="ssum", name="ssum")
+            for c in range(N_SRC):
+                e_tile[i, c] = work.tile([P, PER_SRC], F32, tag="e%d" % c, name="e")
+                nc.scalar.activation(
+                    out=e_tile[i, c][:], in_=s_bank[i, c][:], func=ACT.Exp, bias=bias[i][:, c : c + 1], scale=SCALE, accum_out=ssum[i][:, c : c + 1]
+                )
+
+        def recip(i):
+            rinv[i] = small.tile([P, N_SRC], F32, tag="rinv", name="rinv")
+            nc.vector.reciprocal(out=rinv[i][:], in_=ssum[i][:])
+
+        def weigh(i, c, engine):
+            r = i % ROW_TILES
+            p_tile[i, c] = work.tile([P, PER_SRC], F32, tag="p%d" % c, name="p")
+            eng = nc.gpsimd if engine == "G" else nc.vector
+            eng.tensor_scalar(
+                out=p_tile[i, c][:],
+                in0=e_tile[i, c][:],
+                scalar1=rinv[i][:, c : c + 1],
+                scalar2=lam_f[:, N_SRC * r + c : N_SRC * r + c + 1],
+                op0=ALU.mult,
+                op1=ALU.mult,
+            )
+
+        def turn(i, c):
+            t_bank[i, c] = bank("t%d" % c)
+            for t in range(PACK):
+                nc.tensor.transpose(t_bank[i, c][:, P * t : P * (t + 1)], p_tile[i, c][:, P * t : P * (t + 1)], ident[:])
+
+        def gain(i, c):
+            if c == 0:
+                a_tile[i] = work.tile([P, N_SRC, P, PACK], BF16, tag="a", name="a", align_bytes=64)
+            nc.vector.tensor_tensor(
+                out=a_tile[i][:, c, :, :],
+                in0=t_bank[i, c][:].rearrange("p (t n) -> p n t", t=PACK),
+                in1=g_f[:, PACK * c : PACK * (c + 1)].unsqueeze(1).to_broadcast([P, P, PACK]),
+                op=ALU.mult,
+            )
+
+        def a_quant(i):
+            a_codes[i] = codes.tile([P, N_SRC * P], U32, tag="a_codes", name="a_codes", align_bytes=64)
+            a_scales[i] = codes.tile([P, N_SRC * P], U8, tag="a_scales", name="a_scales", align_bytes=64)
+            nc.vector.quantize_mx(
+                out=a_codes[i][:].bitcast(FP8X4), scales=a_scales[i][:], in_=a_tile[i][:].rearrange("p c n t -> p (c n t)")
+            )
+
+        def mm_out(i):
+            h = i // ROW_TILES
+            o_bank[i] = bank("w0")
+            for c in range(N_SRC):
+                cols = slice(P * c, P * (c + 1))
+                nc.tensor.matmul_mx(
+                    out=o_bank[i][:],
+                    lhsT=a_codes[i][:, cols].bitcast(FP8X4),
+                    lhsT_scale=a_scales[i][:, cols],
+                    rhs=v_codes[h, c][:].bitcast(FP8X4),
+                    rhs_scale=v_scales[h, c][:],
+                    start=(c == 0),
+                    stop=(c == N_SRC - 1),
+                )
+
+        def store(i):
+            h, r = divmod(i, ROW_TILES)
+            res = work.tile([P, V_WIDTH], F32, tag="res", name="res")
+            dst = out[h].rearrange("(p r) e -> p r e", r=ROW_TILES)[:, r, :]
+            if i < UNITS - 1:
+                nc.scalar.copy(out=res[:], in_=o_bank[i][:])
+                nc.sync.dma_start(out=dst, in_=res[:])
+            else:
+                nc.scalar.copy(out=res[:, 0:256], in_=o_bank[i][:, 0:256])
+                nc.sync.dma_start(out=dst[:, 0:256], in_=res[:, 0:256])
+                nc.vector.tensor_copy(out=res[:, 256:512], in_=o_bank[i][:, 256:512])
+                nc.sync.dma_start(out=dst[:, 256:512], in_=res[:, 256:512])
+
+        def head_jobs(h):
+            return [("k", h, 0, 0), ("k", h, 0, 1), ("k", h, 1, 0), ("k", h, 1, 1), ("q", h, 0, 0), ("q", h, 0, 1)]
+
+        j = [("k", 0, 0, 0), ("k", 0, 0, 1), ("q", 0, 0, 0), ("k", 0, 1, 0), ("k", 0, 1, 1), ("q", 0, 0, 1)]
+        job_copy(j[0], "w0", "V")
+        job_copy(j[1], "w1", "S")
+        job_copy(j[2], "t0", "V")
+        job_quant(j[0])
+        job_copy(j[3], "t1", "S")
+        job_quant(j[1])
+        job_quant(j[2])
+        job_copy(j[4], "w0", "V")
+        job_quant(j[3])
+        job_quant(j[4])
+
+        side_copy, side_quant, side_widen, side_inter, side_vq = {}, {}, {}, {}, {}
+        side_copy[-2] = [j[5]]
+        side_quant[-1] = [j[5]]
+        for h in range(1, HEADS):
+            js = head_jobs(h)
+            i0 = ROW_TILES * h - 6
+            for d, part in enumerate((js[0:2], js[2:3], js[3:5], js[5:6])):
+                side_copy.setdefault(i0 + d, []).extend(part)
+                side_quant.setdefault(i0 + d + 1, []).extend(part)
+        for h in range(HEADS):
+            i0 = ROW_TILES * h
+            for c in range(N_SRC):
+                for t in range(PACK):
+                    if h == 0:
+                        side_widen.setdefault(c - 1, []).append((h, c, t, "VV"[c]))
+                    else:
+                        side_widen.setdefault(i0 - 4 + 2 * c + t // 2, []).append((h, c, t, "S"))
+                side_inter.setdefault(max(c, i0 - 1 + c), []).append((h, c))
+                side_vq.setdefault(max(1, i0 + c), []).append((h, c))
+
+        for i in range(-2, UNITS + 2):
+            live = 0 <= i < UNITS
+            prev = 0 <= i - 1 < UNITS
+            nxt = 0 <= i + 1 < UNITS
+            quants = list(side_quant.get(i, []))
+            copies = list(side_copy.get(i, []))
+            if i >= 0:
+                for item in side_widen.get(i, []):
+                    v_widen(*item)
+            if 0 <= i - 2:
+                mm_out(i - 2)
+                store(i - 2)
+            if 0 <= i + 2 < UNITS:
+                mm_scores(i + 2)
+            if nxt:
+                row_max(i + 1, 0)
+                row_max(i + 1, 1)
+            if live:
+                recip(i)
+                weigh(i, 0, "G")
+                weigh(i, 1, "G")
+            for job in copies[:1]:
+                job_copy(job, "w1", "S")
+            if prev:
+                gain(i - 1, 0)
+            for job in quants[:1]:
+                job_quant(job)
+            if nxt:
+                neg_scale(i + 1)
+                exps(i + 1)
+            for n, job in enumerate(copies[1:]):
+                job_copy(job, ("w0", "t0")[n], "S")
+            if live:
+                turn(i, 0)
+                turn(i, 1)
+            if prev:
+                gain(i - 1, 1)
+            for job in quants[1:]:
+                job_quant(job)
+            for h, c in side_inter.get(i, []):
+                if SPLIT:
+                    v_inter(h, c, 0, SPLIT, "V")
+                for lo in range(SPLIT, V_WIDTH, 128):
+                    v_inter(h, c, lo, lo + 128, "G")
+            for h, c in side_vq.get(i, []):
+                v_quant(h, c)
+            if prev:
+                a_quant(i - 1)
+            if i < 0:
+                for item in side_widen.get(i, []):
+                    v_widen(*item)

@@ -21,7 +21,10 @@ P = 128
 PACK = 4
 ROW_TILES = N_POS // P
 UNITS = HEADS * ROW_TILES
-SPLIT = 256
+SI = ((3, 1), (3, 0))
+WIDEN_V = ((0, 1), (0, 2), (0, 3))
+RATE = {-3: 8, -2: 14, -1: 18, 0: 20, 1: 22, 2: 26, 3: 31, 4: 32, 5: 36, 6: 45, 7: 47, 8: 50, 9: 54, 10: 56, 11: 61, 12: 65, 13: 69, 14: 73, 15: 77, 16: 81}
+J0, J1, J2, J3, J4 = 'SSSSS'
 SCALE = 1.0 / math.sqrt(WIDTH)
 
 
@@ -145,6 +148,8 @@ def tile_ipadapterregionaldecoupledcrossattention_kernel(tc, q, k, v_bytes, v_sc
             dst, src = inter[h, c][:, lo:hi, :], wide[h, c][:, :, lo:hi].rearrange("p t n -> p n t")
             if engine == "V":
                 nc.vector.tensor_copy(out=dst, in_=src)
+            elif engine == "S":
+                nc.scalar.copy(out=dst, in_=src)
             else:
                 nc.gpsimd.tensor_scalar(out=dst, in0=src, scalar1=1.0, scalar2=0.0, op0=ALU.mult, op1=ALU.add)
 
@@ -179,7 +184,7 @@ def tile_ipadapterregionaldecoupledcrossattention_kernel(tc, q, k, v_bytes, v_sc
 
         def neg_scale(i):
             bias[i] = small.tile([P, N_SRC], F32, tag="bias", name="bias")
-            nc.vector.tensor_scalar(out=bias[i][:], in0=top[i][:], scalar1=-SCALE, scalar2=None, op0=ALU.mult)
+            nc.scalar.activation(out=bias[i][:], in_=top[i][:], func=ACT.Copy, scale=-SCALE)
 
         def exps(i):
             ssum[i] = small.tile([P, N_SRC], F32, tag="ssum", name="ssum")
@@ -221,11 +226,15 @@ def tile_ipadapterregionaldecoupledcrossattention_kernel(tc, q, k, v_bytes, v_sc
                 op=ALU.mult,
             )
 
-        def a_quant(i):
-            a_codes[i] = codes.tile([P, N_SRC * P], U32, tag="a_codes", name="a_codes", align_bytes=64)
-            a_scales[i] = codes.tile([P, N_SRC * P], U8, tag="a_scales", name="a_scales", align_bytes=64)
+        def a_quant(i, c0, c1):
+            if c0 == 0:
+                a_codes[i] = codes.tile([P, N_SRC * P], U32, tag="a_codes", name="a_codes", align_bytes=64)
+                a_scales[i] = codes.tile([P, N_SRC * P], U8, tag="a_scales", name="a_scales", align_bytes=64)
+            cols = slice(P * c0, P * c1)
             nc.vector.quantize_mx(
-                out=a_codes[i][:].bitcast(FP8X4), scales=a_scales[i][:], in_=a_tile[i][:].rearrange("p c n t -> p (c n t)")
+                out=a_codes[i][:, cols].bitcast(FP8X4),
+                scales=a_scales[i][:, cols],
+                in_=a_tile[i][:, c0:c1, :, :].rearrange("p c n t -> p (c n t)"),
             )
 
         def mm_out(i):
@@ -259,86 +268,98 @@ def tile_ipadapterregionaldecoupledcrossattention_kernel(tc, q, k, v_bytes, v_sc
         def head_jobs(h):
             return [("k", h, 0, 0), ("k", h, 0, 1), ("k", h, 1, 0), ("k", h, 1, 1), ("q", h, 0, 0), ("q", h, 0, 1)]
 
-        j = [("k", 0, 0, 0), ("k", 0, 0, 1), ("q", 0, 0, 0), ("k", 0, 1, 0), ("k", 0, 1, 1), ("q", 0, 0, 1)]
-        job_copy(j[0], "w0", "V")
-        job_copy(j[1], "w1", "S")
-        job_copy(j[2], "t0", "V")
-        job_quant(j[0])
-        job_copy(j[3], "t1", "S")
-        job_quant(j[1])
-        job_quant(j[2])
-        job_copy(j[4], "w0", "V")
-        job_quant(j[3])
-        job_quant(j[4])
+        warm_bank = bank("t1")
+        for n in range(16):
+            nc.tensor.transpose(warm_bank[:, 0:P], ident[:], ident[:])
+        first = [("k", 0, 0, 0), ("k", 0, 0, 1), ("q", 0, 0, 0), ("k", 0, 1, 0), ("k", 0, 1, 1)]
+        job_copy(first[0], "w0", J0)
+        job_copy(first[1], "w1", J1)
+        job_copy(first[2], "t0", J2)
+        job_quant(first[0])
+        job_copy(first[3], "t1", J3)
+        job_quant(first[1])
+        job_quant(first[2])
+        job_copy(first[4], "w0", J4)
+        job_quant(first[3])
+        job_quant(first[4])
+        mm_scores(0)
 
-        side_copy, side_quant, side_widen, side_inter, side_vq = {}, {}, {}, {}, {}
-        side_copy[-2] = [j[5]]
-        side_quant[-1] = [j[5]]
-        for h in range(1, HEADS):
-            js = head_jobs(h)
-            i0 = ROW_TILES * h - 6
-            for d, part in enumerate((js[0:2], js[2:3], js[3:5], js[5:6])):
-                side_copy.setdefault(i0 + d, []).extend(part)
-                side_quant.setdefault(i0 + d + 1, []).extend(part)
+        pieces = [("job", ("q", 0, 0, 1))]
         for h in range(HEADS):
-            i0 = ROW_TILES * h
+            wid = []
             for c in range(N_SRC):
-                for t in range(PACK):
-                    if h == 0:
-                        side_widen.setdefault(c - 1, []).append((h, c, t, "VV"[c]))
-                    else:
-                        side_widen.setdefault(i0 - 4 + 2 * c + t // 2, []).append((h, c, t, "S"))
-                side_inter.setdefault(max(c, i0 - 1 + c), []).append((h, c))
-                side_vq.setdefault(max(1, i0 + c), []).append((h, c))
+                wid += [("widen", (h, c, t)) for t in range(PACK)]
+                if (h, c) in SI:
+                    wid += [("inter", (h, c, lo)) for lo in range(0, V_WIDTH, 128)]
+            nj = [("job", job) for job in head_jobs(h + 1)] if h + 1 < HEADS else []
+            while wid or nj:
+                pieces += wid[:1] + nj[:1]
+                wid, nj = wid[1:], nj[1:]
+        quants, next_quants, inters, next_inters, vqs, next_vqs = [], [], [], [], [], []
+        taken = 0
+        n_jobs = 0
 
-        for i in range(-2, UNITS + 2):
+        def piece(kind, item):
+            if kind == "job":
+                job_copy(item, ("w1", "w0")[n_jobs % 2], "S")
+                next_quants.append(item)
+            elif kind == "widen":
+                h, c, t = item
+                v_widen(h, c, t, "V" if (h, t) in WIDEN_V else "S")
+                if t == PACK - 1 and (h, c) not in SI:
+                    next_inters.append((h, c))
+            else:
+                h, c, lo = item
+                v_inter(h, c, lo, lo + 128, "S")
+                if lo + 128 == V_WIDTH:
+                    next_vqs.append((h, c))
+
+        for i in range(-3, UNITS + 1):
             live = 0 <= i < UNITS
             prev = 0 <= i - 1 < UNITS
-            nxt = 0 <= i + 1 < UNITS
-            quants = list(side_quant.get(i, []))
-            copies = list(side_copy.get(i, []))
-            if i >= 0:
-                for item in side_widen.get(i, []):
-                    v_widen(*item)
-            if 0 <= i - 2:
-                mm_out(i - 2)
-                store(i - 2)
-            if 0 <= i + 2 < UNITS:
-                mm_scores(i + 2)
-            if nxt:
-                row_max(i + 1, 0)
-                row_max(i + 1, 1)
+            last = i == UNITS - 1
+            upto = min(len(pieces), RATE[i])
+            todo = pieces[taken:upto]
+            taken = max(taken, upto)
             if live:
                 recip(i)
-                weigh(i, 0, "G")
-                weigh(i, 1, "G")
-            for job in copies[:1]:
-                job_copy(job, "w1", "S")
-            if prev:
-                gain(i - 1, 0)
-            for job in quants[:1]:
-                job_quant(job)
-            if nxt:
+                weigh(i, 0, "V" if last else "G")
+                weigh(i, 1, "V" if last else "G")
+            if 0 <= i + 1 < UNITS:
                 neg_scale(i + 1)
                 exps(i + 1)
-            for n, job in enumerate(copies[1:]):
-                job_copy(job, ("w0", "t0")[n], "S")
+            if 0 <= i + 2 < UNITS:
+                row_max(i + 2, 0)
+                row_max(i + 2, 1)
+            if 0 <= i - 2:
+                store(i - 2)
+            for kind, item in todo:
+                piece(kind, item)
+                n_jobs += kind == "job"
+            if prev:
+                gain(i - 1, 0)
+                if i == UNITS:
+                    a_quant(i - 1, 0, 1)
+                gain(i - 1, 1)
             if live:
                 turn(i, 0)
                 turn(i, 1)
-            if prev:
-                gain(i - 1, 1)
-            for job in quants[1:]:
+            for job in quants:
                 job_quant(job)
-            for h, c in side_inter.get(i, []):
-                if SPLIT:
-                    v_inter(h, c, 0, SPLIT, "V")
-                for lo in range(SPLIT, V_WIDTH, 128):
-                    v_inter(h, c, lo, lo + 128, "G")
-            for h, c in side_vq.get(i, []):
+            for h, c in vqs:
                 v_quant(h, c)
+            if 0 < i + 3 < UNITS:
+                mm_scores(i + 3)
             if prev:
-                a_quant(i - 1)
-            if i < 0:
-                for item in side_widen.get(i, []):
-                    v_widen(*item)
+                if i == UNITS:
+                    a_quant(i - 1, 1, 2)
+                else:
+                    a_quant(i - 1, 0, 2)
+                mm_out(i - 1)
+            for h, c in inters:
+                for lo in range(0, V_WIDTH, 256):
+                    v_inter(h, c, lo, lo + 256, "V")
+            quants, next_quants = next_quants, []
+            vqs, next_vqs = list(inters) + next_vqs, []
+            inters, next_inters = next_inters, []
+        store(UNITS - 1)

@@ -22,9 +22,11 @@ PACK = 4
 ROW_TILES = N_POS // P
 UNITS = HEADS * ROW_TILES
 SI = ((3, 1), (3, 0))
-WIDEN_V = ((0, 1), (0, 2), (0, 3))
-RATE = {-3: 8, -2: 14, -1: 18, 0: 20, 1: 22, 2: 26, 3: 31, 4: 32, 5: 36, 6: 45, 7: 47, 8: 50, 9: 54, 10: 56, 11: 61, 12: 65, 13: 69, 14: 73, 15: 77, 16: 81}
-J0, J1, J2, J3, J4 = 'SSSSS'
+WIDEN_V = ((0, 1), (0, 3), (0, 2), (2, 1), (2, 3))
+RATE = {-3: 8, -2: 15, -1: 16, 0: 18, 1: 22, 2: 26, 3: 31, 4: 32, 5: 36, 6: 46, 7: 49, 8: 53, 9: 55, 10: 56, 11: 67, 12: 67, 13: 67, 14: 67, 15: 67, 16: 67}
+JS = 'SVSSS'
+WARM, PADP, PADJ, PADT = 832, 0, 64, 192
+OUT_FIRST = False
 SCALE = 1.0 / math.sqrt(WIDTH)
 
 
@@ -98,10 +100,15 @@ def tile_ipadapterregionaldecoupledcrossattention_kernel(tc, q, k, v_bytes, v_sc
         q_codes, q_scales, k_codes, k_scales, v_codes, v_scales = {}, {}, {}, {}, {}, {}
         grouped = {}
 
-        def job_copy(job, tag, engine):
+        def dummy(b, n):
+            for n0 in range(0, n, 128):
+                nc.tensor.matmul(b[:, 0 : min(128, n - n0)], ident[:], ident[:, 0 : min(128, n - n0)], start=True, stop=True)
+
+        def job_copy(job, tag, engine, pad=0):
             kind, h, c, half = job
             src = q_raw[h] if kind == "q" else k_raw[h, c]
             b = bank(tag)
+            dummy(b, pad)
             view = b[:].rearrange("p (s u r) -> p s u r", s=2, u=2)
             for s in range(2):
                 words = src[:, 2 * half + s, :].bitcast(F32)
@@ -211,8 +218,9 @@ def tile_ipadapterregionaldecoupledcrossattention_kernel(tc, q, k, v_bytes, v_sc
                 op1=ALU.mult,
             )
 
-        def turn(i, c):
+        def turn(i, c, pad=0):
             t_bank[i, c] = bank("t%d" % c)
+            dummy(t_bank[i, c], pad)
             for t in range(PACK):
                 nc.tensor.transpose(t_bank[i, c][:, P * t : P * (t + 1)], p_tile[i, c][:, P * t : P * (t + 1)], ident[:])
 
@@ -228,8 +236,8 @@ def tile_ipadapterregionaldecoupledcrossattention_kernel(tc, q, k, v_bytes, v_sc
 
         def a_quant(i, c0, c1):
             if c0 == 0:
-                a_codes[i] = codes.tile([P, N_SRC * P], U32, tag="a_codes", name="a_codes", align_bytes=64)
-                a_scales[i] = codes.tile([P, N_SRC * P], U8, tag="a_scales", name="a_scales", align_bytes=64)
+                a_codes[i] = codes.tile([P, N_SRC * P], U32, tag="a_codes", name="a_codes", bufs=3, align_bytes=64)
+                a_scales[i] = codes.tile([P, N_SRC * P], U8, tag="a_scales", name="a_scales", bufs=3, align_bytes=64)
             cols = slice(P * c0, P * c1)
             nc.vector.quantize_mx(
                 out=a_codes[i][:, cols].bitcast(FP8X4),
@@ -268,18 +276,16 @@ def tile_ipadapterregionaldecoupledcrossattention_kernel(tc, q, k, v_bytes, v_sc
         def head_jobs(h):
             return [("k", h, 0, 0), ("k", h, 0, 1), ("k", h, 1, 0), ("k", h, 1, 1), ("q", h, 0, 0), ("q", h, 0, 1)]
 
-        warm_bank = bank("t1")
-        for n in range(16):
-            nc.tensor.transpose(warm_bank[:, 0:P], ident[:], ident[:])
+        dummy(bank("t1"), WARM)
         first = [("k", 0, 0, 0), ("k", 0, 0, 1), ("q", 0, 0, 0), ("k", 0, 1, 0), ("k", 0, 1, 1)]
-        job_copy(first[0], "w0", J0)
-        job_copy(first[1], "w1", J1)
-        job_copy(first[2], "t0", J2)
+        job_copy(first[0], "w0", JS[0], PADP)
+        job_copy(first[1], "w1", JS[1], PADP)
+        job_copy(first[2], "t0", JS[2], PADP)
         job_quant(first[0])
-        job_copy(first[3], "t1", J3)
+        job_copy(first[3], "t1", JS[3], PADP)
         job_quant(first[1])
         job_quant(first[2])
-        job_copy(first[4], "w0", J4)
+        job_copy(first[4], "w0", JS[4], PADP)
         job_quant(first[3])
         job_quant(first[4])
         mm_scores(0)
@@ -297,11 +303,10 @@ def tile_ipadapterregionaldecoupledcrossattention_kernel(tc, q, k, v_bytes, v_sc
                 wid, nj = wid[1:], nj[1:]
         quants, next_quants, inters, next_inters, vqs, next_vqs = [], [], [], [], [], []
         taken = 0
-        n_jobs = 0
 
-        def piece(kind, item):
+        def piece(kind, item, tag, pad):
             if kind == "job":
-                job_copy(item, ("w1", "w0")[n_jobs % 2], "S")
+                job_copy(item, tag, "S", pad)
                 next_quants.append(item)
             elif kind == "widen":
                 h, c, t = item
@@ -321,45 +326,56 @@ def tile_ipadapterregionaldecoupledcrossattention_kernel(tc, q, k, v_bytes, v_sc
             upto = min(len(pieces), RATE[i])
             todo = pieces[taken:upto]
             taken = max(taken, upto)
+            jobs = [x for x in todo if x[0] == "job"]
+            others = [x for x in todo if x[0] != "job"]
+            if 0 <= i - 2:
+                mm_out(i - 2)
             if live:
                 recip(i)
                 weigh(i, 0, "V" if last else "G")
                 weigh(i, 1, "V" if last else "G")
+            if 0 <= i - 2 and OUT_FIRST:
+                store(i - 2)
             if 0 <= i + 1 < UNITS:
                 neg_scale(i + 1)
                 exps(i + 1)
             if 0 <= i + 2 < UNITS:
                 row_max(i + 2, 0)
                 row_max(i + 2, 1)
-            if 0 <= i - 2:
+            if 0 <= i - 2 and not OUT_FIRST:
                 store(i - 2)
-            for kind, item in todo:
-                piece(kind, item)
-                n_jobs += kind == "job"
+            for kind, item in others[:1]:
+                piece(kind, item, None, 0)
+            for n, (kind, item) in enumerate(jobs[:1]):
+                piece(kind, item, "w1", PADP if i < 0 else PADJ)
             if prev:
                 gain(i - 1, 0)
                 if i == UNITS:
                     a_quant(i - 1, 0, 1)
                 gain(i - 1, 1)
-            if live:
-                turn(i, 0)
-                turn(i, 1)
             for job in quants:
                 job_quant(job)
             for h, c in vqs:
                 v_quant(h, c)
             if 0 < i + 3 < UNITS:
                 mm_scores(i + 3)
+            for n, (kind, item) in enumerate(jobs[1:]):
+                piece(kind, item, ("w0", "w1")[n % 2], PADP if i < 0 else 0)
+            for kind, item in others[1:]:
+                piece(kind, item, None, 0)
+            if live:
+                turn(i, 0, PADT if jobs or i < 10 else 0)
+                turn(i, 1)
             if prev:
                 if i == UNITS:
                     a_quant(i - 1, 1, 2)
                 else:
                     a_quant(i - 1, 0, 2)
-                mm_out(i - 1)
             for h, c in inters:
                 for lo in range(0, V_WIDTH, 256):
                     v_inter(h, c, lo, lo + 256, "V")
             quants, next_quants = next_quants, []
             vqs, next_vqs = list(inters) + next_vqs, []
             inters, next_inters = next_inters, []
+        mm_out(UNITS - 1)
         store(UNITS - 1)

@@ -22,11 +22,13 @@ PACK = 4
 ROW_TILES = N_POS // P
 UNITS = HEADS * ROW_TILES
 SI = ((3, 1), (3, 0))
-WIDEN_V = ((0, 1), (0, 3), (0, 2), (2, 1), (2, 3))
-RATE = {-3: 8, -2: 15, -1: 16, 0: 18, 1: 22, 2: 26, 3: 31, 4: 32, 5: 36, 6: 46, 7: 49, 8: 53, 9: 55, 10: 56, 11: 67, 12: 67, 13: 67, 14: 67, 15: 67, 16: 67}
-JS = 'SVSSS'
-WARM, PADP, PADJ, PADT = 832, 0, 64, 192
+WIDEN_V = ((0, 1), (0, 2), (2, 1), (3, 0), (0, 3), (1, 3), (0, 0))
+RATE = {-3: 8, -2: 15, -1: 19, 0: 22, 1: 24, 2: 29, 3: 33, 4: 36, 5: 40, 6: 45, 7: 48, 8: 50, 9: 53, 10: 56, 11: 60, 12: 62, 13: 64, 14: 66, 15: 68, 16: 70}
+JS = 'SVSVS'
+WARM, PADP, PADJ, PADT, PADU, PADS = 640, 0, 64, 192, 0, 0
 OUT_FIRST = False
+NG = 2
+LASTW = "GG"
 SCALE = 1.0 / math.sqrt(WIDTH)
 
 
@@ -150,9 +152,13 @@ def tile_ipadapterregionaldecoupledcrossattention_kernel(tc, q, k, v_bytes, v_sc
                 nc.vector.tensor_scalar(out=dst, in0=src, scalar1=sc, scalar2=None, op0=ALU.mult)
 
         def v_inter(h, c, lo, hi, engine):
-            if lo == 0:
+            if (h, c) not in inter:
                 inter[h, c] = work.tile([P, V_WIDTH, PACK], BF16, tag="inter", name="inter", align_bytes=64)
-            dst, src = inter[h, c][:, lo:hi, :], wide[h, c][:, :, lo:hi].rearrange("p t n -> p n t")
+            dst = inter[h, c][:, lo:hi, :]
+            src = wide[h, c][:, :, lo:hi].rearrange("p t n -> p n t")
+            if engine != "G":
+                dst = dst.rearrange("p (n i) t -> p n t i", i=4)
+                src = src.rearrange("p (n i) t -> p n t i", i=4)
             if engine == "V":
                 nc.vector.tensor_copy(out=dst, in_=src)
             elif engine == "S":
@@ -169,11 +175,12 @@ def tile_ipadapterregionaldecoupledcrossattention_kernel(tc, q, k, v_bytes, v_sc
 
         s_bank, e_tile, p_tile, t_bank, a_tile, a_codes, a_scales, top, ssum, rinv, bias, o_bank = {}, {}, {}, {}, {}, {}, {}, {}, {}, {}, {}, {}
 
-        def mm_scores(i):
+        def mm_scores(i, pad=0):
             h, r = divmod(i, ROW_TILES)
             cols = slice(P * r, P * (r + 1))
             for c in range(N_SRC):
                 s_bank[i, c] = bank("s%d" % (2 * (i % 2) + c))
+                dummy(s_bank[i, c], pad if c == 0 else 0)
                 nc.tensor.matmul_mx(
                     out=s_bank[i, c][:],
                     lhsT=q_codes[h][:, cols].bitcast(FP8X4),
@@ -201,9 +208,11 @@ def tile_ipadapterregionaldecoupledcrossattention_kernel(tc, q, k, v_bytes, v_sc
                     out=e_tile[i, c][:], in_=s_bank[i, c][:], func=ACT.Exp, bias=bias[i][:, c : c + 1], scale=SCALE, accum_out=ssum[i][:, c : c + 1]
                 )
 
-        def recip(i):
+        def recip(i, apart):
             rinv[i] = small.tile([P, N_SRC], F32, tag="rinv", name="rinv")
-            nc.vector.reciprocal(out=rinv[i][:], in_=ssum[i][:])
+            for c in range(N_SRC) if apart else (slice(0, N_SRC),):
+                cols = slice(c, c + 1) if apart else c
+                nc.vector.reciprocal(out=rinv[i][:, cols], in_=ssum[i][:, cols])
 
         def weigh(i, c, engine):
             r = i % ROW_TILES
@@ -289,6 +298,8 @@ def tile_ipadapterregionaldecoupledcrossattention_kernel(tc, q, k, v_bytes, v_sc
         job_quant(first[3])
         job_quant(first[4])
         mm_scores(0)
+        row_max(0, 0)
+        row_max(0, 1)
 
         pieces = [("job", ("q", 0, 0, 1))]
         for h in range(HEADS):
@@ -301,6 +312,7 @@ def tile_ipadapterregionaldecoupledcrossattention_kernel(tc, q, k, v_bytes, v_sc
             while wid or nj:
                 pieces += wid[:1] + nj[:1]
                 wid, nj = wid[1:], nj[1:]
+        by_g = set()
         quants, next_quants, inters, next_inters, vqs, next_vqs = [], [], [], [], [], []
         taken = 0
 
@@ -331,15 +343,21 @@ def tile_ipadapterregionaldecoupledcrossattention_kernel(tc, q, k, v_bytes, v_sc
             if 0 <= i - 2:
                 mm_out(i - 2)
             if live:
-                recip(i)
-                weigh(i, 0, "V" if last else "G")
-                weigh(i, 1, "V" if last else "G")
+                recip(i, False)
+                weigh(i, 0, LASTW[0] if last else "G")
+                weigh(i, 1, LASTW[1] if last else "G")
+            for h, c in inters[:NG]:
+                v_inter(h, c, 0, 128, "G")
+            for h, c in vqs:
+                if (h, c) in by_g and NG > 1:
+                    v_inter(h, c, 128, 256, "G")
+            by_g.update(inters)
             if 0 <= i - 2 and OUT_FIRST:
                 store(i - 2)
             if 0 <= i + 1 < UNITS:
                 neg_scale(i + 1)
                 exps(i + 1)
-            if 0 <= i + 2 < UNITS:
+            if 0 < i + 2 < UNITS:
                 row_max(i + 2, 0)
                 row_max(i + 2, 1)
             if 0 <= i - 2 and not OUT_FIRST:
@@ -358,22 +376,25 @@ def tile_ipadapterregionaldecoupledcrossattention_kernel(tc, q, k, v_bytes, v_sc
             for h, c in vqs:
                 v_quant(h, c)
             if 0 < i + 3 < UNITS:
-                mm_scores(i + 3)
+                mm_scores(i + 3, PADS)
             for n, (kind, item) in enumerate(jobs[1:]):
                 piece(kind, item, ("w0", "w1")[n % 2], PADP if i < 0 else 0)
             for kind, item in others[1:]:
                 piece(kind, item, None, 0)
             if live:
                 turn(i, 0, PADT if jobs or i < 10 else 0)
-                turn(i, 1)
+                turn(i, 1, PADU)
             if prev:
                 if i == UNITS:
                     a_quant(i - 1, 1, 2)
                 else:
                     a_quant(i - 1, 0, 2)
             for h, c in inters:
-                for lo in range(0, V_WIDTH, 256):
-                    v_inter(h, c, lo, lo + 256, "V")
+                if NG == 0:
+                    v_inter(h, c, 0, 256, "V")
+                if NG == 1:
+                    v_inter(h, c, 128, 256, "V")
+                v_inter(h, c, 256, 512, "V")
             quants, next_quants = next_quants, []
             vqs, next_vqs = list(inters) + next_vqs, []
             inters, next_inters = next_inters, []

import math
from contextlib import ExitStack

import concourse.mybir as mybir
from concourse.masks import make_identity

HEADS, N_POS, WIDTH, N_SRC, PER_SRC, V_WIDTH = 4, 512, 512, 2, 512, 512
FLOPS = 2 * HEADS * N_POS * N_SRC * PER_SRC * (WIDTH + V_WIDTH)

F32 = mybir.dt.float32
BF16 = mybir.dt.bfloat16
U32 = mybir.dt.uint32
U8 = mybir.dt.uint8
E4M3 = mybir.dt.float8_e4m3fn
FP8X4 = mybir.dt.float8_e4m3fn_x4
ACT = mybir.ActivationFunctionType
ALU = mybir.AluOpType
AX = mybir.AxisListType

P = 128
PACK = 4
ROW_TILES = N_POS // P
UNITS = HEADS * ROW_TILES
SI = ((3, 1), (3, 0))
WIDEN_V = ((0, 1), (0, 2), (2, 1), (3, 0), (0, 3), (1, 3), (0, 0))
RATE = {-3: 8, -2: 15, -1: 19, 0: 22, 1: 24, 2: 29, 3: 33, 4: 36, 5: 40, 6: 45, 7: 48, 8: 50, 9: 53, 10: 56, 11: 60, 12: 62, 13: 64, 14: 66, 15: 68, 16: 70}
JS = 'SVSVS'
WARM, PADP, PADJ, PADT, PADU, PADS = 640, 0, 64, 192, 0, 0
OUT_FIRST = False
NG = 2
LASTW = "GG"
SCALE = 1.0 / math.sqrt(WIDTH)


def tile_ipadapterregionaldecoupledcrossattention_kernel(tc, q, k, v_bytes, v_scale, g, lam, out):
    nc = tc.nc
    with ExitStack() as ctx:
        const = ctx.enter_context(tc.tile_pool(name="const", bufs=1))
        raw = ctx.enter_context(tc.tile_pool(name="raw", bufs=1))
        work = ctx.enter_context(tc.tile_pool(name="work", bufs=3))
        small = ctx.enter_context(tc.tile_pool(name="small", bufs=4))
        codes = ctx.enter_context(tc.tile_pool(name="codes", bufs=2))
        psum = ctx.enter_context(tc.psum_pool(name="psum", bufs=1))
        ctx.enter_context(tc.manual_schedule())

        def bank(tag):
            t = psum.tile([P, 512], F32, tag=tag, name=tag)
            return t

        q_raw, k_raw, v_raw = {}, {}, {}
        for h in range(HEADS):
            q_raw[h] = raw.tile([P, ROW_TILES, WIDTH], BF16, name="q_raw%d" % h)
            for c in range(N_SRC):
                k_raw[h, c] = raw.tile([P, PACK, WIDTH], BF16, name="k_raw%d_%d" % (h, c))
            v_raw[h] = raw.tile([P, N_SRC, PACK, V_WIDTH], U8, name="v_raw%d" % h)

        def load_q(h, r0, r1):
            nc.sync.dma_start(out=q_raw[h][:, r0:r1, :], in_=q[h].rearrange("(p r) e -> p r e", r=ROW_TILES)[:, r0:r1, :])

        def load_k(h, c, t0, t1):
            nc.sync.dma_start(
                out=k_raw[h, c][:, t0:t1, :],
                in_=k[h, c * PER_SRC : (c + 1) * PER_SRC, :].rearrange("(p t) e -> p t e", t=PACK)[:, t0:t1, :],
            )

        def load_v(h):
            nc.sync.dma_start(out=v_raw[h][:], in_=v_bytes[h].rearrange("(c p t) n -> p c t n", p=P, t=PACK))

        load_k(0, 0, 0, 2)
        load_k(0, 0, 2, 4)
        load_q(0, 0, 2)
        load_k(0, 1, 0, 2)
        load_k(0, 1, 2, 4)
        load_q(0, 2, 4)
        load_k(1, 0, 0, 4)
        load_v(0)
        for h in range(1, HEADS):
            if h > 1:
                load_k(h, 0, 0, 4)
            load_k(h, 1, 0, 4)
            load_q(h, 0, 4)
            load_v(h)

        v_sc = const.tile([P, N_SRC * PACK], F32)
        g_bf = const.tile([P, N_SRC * PACK], BF16)
        lam_bf = const.tile([P, ROW_TILES * N_SRC], BF16)
        nc.scalar.dma_start(out=v_sc[:].rearrange("p (c t) -> p c t", t=PACK), in_=v_scale.rearrange("o (c p t) u -> p (o c) (t u)", p=P, t=PACK))
        nc.scalar.dma_start(out=g_bf[:].rearrange("p (c t) -> p c t", t=PACK), in_=g.rearrange("(c p t) -> p c t", p=P, t=PACK))
        nc.scalar.dma_start(out=lam_bf[:], in_=lam.rearrange("(p r) c -> p (r c)", r=ROW_TILES))

        warm = const.tile([P, 1], F32)
        nc.gpsimd.memset(warm[:], 0.0)
        ident = const.tile([P, P], F32)
        make_identity(nc, ident[:])
        warm_out = const.tile([P, 1], F32)
        nc.scalar.activation(out=warm_out[:], in_=warm[:], func=ACT.Exp)
        g_f = const.tile([P, N_SRC * PACK], F32)
        nc.gpsimd.tensor_copy(out=g_f[:], in_=g_bf[:])
        lam_f = const.tile([P, ROW_TILES * N_SRC], F32)
        nc.gpsimd.tensor_copy(out=lam_f[:], in_=lam_bf[:])

        q_codes, q_scales, k_codes, k_scales, v_codes, v_scales = {}, {}, {}, {}, {}, {}
        grouped = {}

        def dummy(b, n):
            for n0 in range(0, n, 128):
                nc.tensor.matmul(b[:, 0 : min(128, n - n0)], ident[:], ident[:, 0 : min(128, n - n0)], start=True, stop=True)

        def job_copy(job, tag, engine, pad=0):
            kind, h, c, half = job
            src = q_raw[h] if kind == "q" else k_raw[h, c]
            b = bank(tag)
            dummy(b, pad)
            view = b[:].rearrange("p (s u r) -> p s u r", s=2, u=2)
            for s in range(2):
                words = src[:, 2 * half + s, :].bitcast(F32)
                for u in range(2):
                    nc.tensor.transpose(view[:, s, u, :], words[:, u : WIDTH // 2 : 2], ident[:])
            xg = work.tile([P, 1024], BF16, tag="xg", name="xg", align_bytes=64)
            grouped[job] = xg
            dst = xg[:].bitcast(F32).rearrange("p (s r u) -> p s r u", s=2, u=2)
            srcv = view.rearrange("p s u r -> p s r u")
            if engine == "S":
                nc.scalar.copy(out=dst, in_=srcv)
            else:
                nc.vector.tensor_copy(out=dst, in_=srcv)

        def job_quant(job):
            kind, h, c, half = job
            if kind == "q":
                if half == 0:
                    q_codes[h] = codes.tile([P, N_POS], U32, tag="q_codes", name="q_codes", align_bytes=64)
                    q_scales[h] = codes.tile([P, N_POS], U8, tag="q_scales", name="q_scales", align_bytes=64)
                cc, ss = q_codes[h], q_scales[h]
            else:
                if half == 0:
                    k_codes[h, c] = codes.tile([P, PER_SRC], U32, tag="k_codes%d" % c, name="k_codes", align_bytes=64)
                    k_scales[h, c] = codes.tile([P, PER_SRC], U8, tag="k_scales%d" % c, name="k_scales", align_bytes=64)
                cc, ss = k_codes[h, c], k_scales[h, c]
            cols = slice(256 * half, 256 * (half + 1))
            nc.vector.quantize_mx(out=cc[:, cols].bitcast(FP8X4), scales=ss[:, cols], in_=grouped[job][:])

        wide, inter = {}, {}

        def v_widen(h, c, t, engine="S"):
            if t == 0:
                wide[h, c] = work.tile([P, PACK, V_WIDTH], BF16, tag="wide", name="wide")
            dst, src, sc = wide[h, c][:, t, :], v_raw[h][:, c, t, :].bitcast(E4M3), v_sc[:, PACK * c + t : PACK * c + t + 1]
            if engine == "S":
                nc.scalar.activation(out=dst, in_=src, func=ACT.Copy, scale=sc)
            else:
                nc.vector.tensor_scalar(out=dst, in0=src, scalar1=sc, scalar2=None, op0=ALU.mult)

        def v_inter(h, c, lo, hi, engine):
            if (h, c) not in inter:
                inter[h, c] = work.tile([P, V_WIDTH, PACK], BF16, tag="inter", name="inter", align_bytes=64)
            dst = inter[h, c][:, lo:hi, :]
            src = wide[h, c][:, :, lo:hi].rearrange("p t n -> p n t")
            if engine != "G":
                dst = dst.rearrange("p (n i) t -> p n t i", i=4)
                src = src.rearrange("p (n i) t -> p n t i", i=4)
            if engine == "V":
                nc.vector.tensor_copy(out=dst, in_=src)
            elif engine == "S":
                nc.scalar.copy(out=dst, in_=src)
            else:
                nc.gpsimd.tensor_scalar(out=dst, in0=src, scalar1=1.0, scalar2=0.0, op0=ALU.mult, op1=ALU.add)

        def v_quant(h, c):
            v_codes[h, c] = codes.tile([P, V_WIDTH], U32, tag="v_codes%d" % c, name="v_codes", align_bytes=64)
            v_scales[h, c] = codes.tile([P, V_WIDTH], U8, tag="v_scales%d" % c, name="v_scales", align_bytes=64)
            nc.vector.quantize_mx(
                out=v_codes[h, c][:].bitcast(FP8X4), scales=v_scales[h, c][:], in_=inter[h, c][:].rearrange("p n t -> p (n t)")
            )

        s_bank, e_tile, p_tile, t_bank, a_tile, a_codes, a_scales, top, ssum, rinv, bias, o_bank = {}, {}, {}, {}, {}, {}, {}, {}, {}, {}, {}, {}

        def mm_scores(i, pad=0):
            h, r = divmod(i, ROW_TILES)
            cols = slice(P * r, P * (r + 1))
            for c in range(N_SRC):
                s_bank[i, c] = bank("s%d" % (2 * (i % 2) + c))
                dummy(s_bank[i, c], pad if c == 0 else 0)
                nc.tensor.matmul_mx(
                    out=s_bank[i, c][:],
                    lhsT=q_codes[h][:, cols].bitcast(FP8X4),
                    lhsT_scale=q_scales[h][:, cols],
                    rhs=k_codes[h, c][:].bitcast(FP8X4),
                    rhs_scale=k_scales[h, c][:],
                    start=True,
                    stop=True,
                )

        def row_max(i, c):
            if c == 0:
                top[i] = small.tile([P, N_SRC], F32, tag="top", name="top")
            nc.vector.reduce_max(out=top[i][:, c : c + 1], in_=s_bank[i, c][:], axis=AX.X)

        def neg_scale(i):
            bias[i] = small.tile([P, N_SRC], F32, tag="bias", name="bias")
            nc.scalar.activation(out=bias[i][:], in_=top[i][:], func=ACT.Copy, scale=-SCALE)

        def exps(i):
            ssum[i] = small.tile([P, N_SRC], F32, tag="ssum", name="ssum")
            for c in range(N_SRC):
                e_tile[i, c] = work.tile([P, PER_SRC], F32, tag="e%d" % c, name="e")
                nc.scalar.activation(
                    out=e_tile[i, c][:], in_=s_bank[i, c][:], func=ACT.Exp, bias=bias[i][:, c : c + 1], scale=SCALE, accum_out=ssum[i][:, c : c + 1]
                )

        def recip(i, apart):
            rinv[i] = small.tile([P, N_SRC], F32, tag="rinv", name="rinv")
            for c in range(N_SRC) if apart else (slice(0, N_SRC),):
                cols = slice(c, c + 1) if apart else c
                nc.vector.reciprocal(out=rinv[i][:, cols], in_=ssum[i][:, cols])

        def weigh(i, c, engine):
            r = i % ROW_TILES
            p_tile[i, c] = work.tile([P, PER_SRC], F32, tag="p%d" % c, name="p")
            eng = nc.gpsimd if engine == "G" else nc.vector
            eng.tensor_scalar(
                out=p_tile[i, c][:],
                in0=e_tile[i, c][:],
                scalar1=rinv[i][:, c : c + 1],
                scalar2=lam_f[:, N_SRC * r + c : N_SRC * r + c + 1],
                op0=ALU.mult,
                op1=ALU.mult,
            )

        def turn(i, c, pad=0):
            t_bank[i, c] = bank("t%d" % c)
            dummy(t_bank[i, c], pad)
            for t in range(PACK):
                nc.tensor.transpose(t_bank[i, c][:, P * t : P * (t + 1)], p_tile[i, c][:, P * t : P * (t + 1)], ident[:])

        def gain(i, c):
            if c == 0:
                a_tile[i] = work.tile([P, N_SRC, P, PACK], BF16, tag="a", name="a", align_bytes=64)
            nc.vector.tensor_tensor(
                out=a_tile[i][:, c, :, :],
                in0=t_bank[i, c][:].rearrange("p (t n) -> p n t", t=PACK),
                in1=g_f[:, PACK * c : PACK * (c + 1)].unsqueeze(1).to_broadcast([P, P, PACK]),
                op=ALU.mult,
            )

        def a_quant(i, c0, c1):
            if c0 == 0:
                a_codes[i] = codes.tile([P, N_SRC * P], U32, tag="a_codes", name="a_codes", bufs=3, align_bytes=64)
                a_scales[i] = codes.tile([P, N_SRC * P], U8, tag="a_scales", name="a_scales", bufs=3, align_bytes=64)
            cols = slice(P * c0, P * c1)
            nc.vector.quantize_mx(
                out=a_codes[i][:, cols].bitcast(FP8X4),
                scales=a_scales[i][:, cols],
                in_=a_tile[i][:, c0:c1, :, :].rearrange("p c n t -> p (c n t)"),
            )

        def mm_out(i):
            h = i // ROW_TILES
            o_bank[i] = bank("w0")
            for c in range(N_SRC):
                cols = slice(P * c, P * (c + 1))
                nc.tensor.matmul_mx(
                    out=o_bank[i][:],
                    lhsT=a_codes[i][:, cols].bitcast(FP8X4),
                    lhsT_scale=a_scales[i][:, cols],
                    rhs=v_codes[h, c][:].bitcast(FP8X4),
                    rhs_scale=v_scales[h, c][:],
                    start=(c == 0),
                    stop=(c == N_SRC - 1),
                )

        def store(i):
            h, r = divmod(i, ROW_TILES)
            res = work.tile([P, V_WIDTH], F32, tag="res", name="res")
            dst = out[h].rearrange("(p r) e -> p r e", r=ROW_TILES)[:, r, :]
            if i < UNITS - 1:
                nc.scalar.copy(out=res[:], in_=o_bank[i][:])
                nc.sync.dma_start(out=dst, in_=res[:])
            else:
                nc.scalar.copy(out=res[:, 0:256], in_=o_bank[i][:, 0:256])
                nc.sync.dma_start(out=dst[:, 0:256], in_=res[:, 0:256])
                nc.vector.tensor_copy(out=res[:, 256:512], in_=o_bank[i][:, 256:512])
                nc.sync.dma_start(out=dst[:, 256:512], in_=res[:, 256:512])

        def head_jobs(h):
            return [("k", h, 0, 0), ("k", h, 0, 1), ("k", h, 1, 0), ("k", h, 1, 1), ("q", h, 0, 0), ("q", h, 0, 1)]

        dummy(bank("t1"), WARM)
        first = [("k", 0, 0, 0), ("k", 0, 0, 1), ("q", 0, 0, 0), ("k", 0, 1, 0), ("k", 0, 1, 1)]
        job_copy(first[0], "w0", JS[0], PADP)
        job_copy(first[1], "w1", JS[1], PADP)
        job_copy(first[2], "t0", JS[2], PADP)
        job_quant(first[0])
        job_copy(first[3], "t1", JS[3], PADP)
        job_quant(first[1])
        job_quant(first[2])
        job_copy(first[4], "w0", JS[4], PADP)
        job_quant(first[3])
        job_quant(first[4])
        mm_scores(0)
        row_max(0, 0)
        row_max(0, 1)

        pieces = [("job", ("q", 0, 0, 1))]
        for h in range(HEADS):
            wid = []
            for c in range(N_SRC):
                wid += [("widen", (h, c, t)) for t in range(PACK)]
                if (h, c) in SI:
                    wid += [("inter", (h, c, lo)) for lo in range(0, V_WIDTH, 128)]
            nj = [("job", job) for job in head_jobs(h + 1)] if h + 1 < HEADS else []
            while wid or nj:
                pieces += wid[:1] + nj[:1]
                wid, nj = wid[1:], nj[1:]
        by_g = set()
        quants, next_quants, inters, next_inters, vqs, next_vqs = [], [], [], [], [], []
        taken = 0

        def piece(kind, item, tag, pad):
            if kind == "job":
                job_copy(item, tag, "S", pad)
                next_quants.append(item)
            elif kind == "widen":
                h, c, t = item
                v_widen(h, c, t, "V" if (h, t) in WIDEN_V else "S")
                if t == PACK - 1 and (h, c) not in SI:
                    next_inters.append((h, c))
            else:
                h, c, lo = item
                v_inter(h, c, lo, lo + 128, "S")
                if lo + 128 == V_WIDTH:
                    next_vqs.append((h, c))

        for i in range(-3, UNITS + 1):
            live = 0 <= i < UNITS
            prev = 0 <= i - 1 < UNITS
            last = i == UNITS - 1
            upto = min(len(pieces), RATE[i])
            todo = pieces[taken:upto]
            taken = max(taken, upto)
            jobs = [x for x in todo if x[0] == "job"]
            others = [x for x in todo if x[0] != "job"]
            if 0 <= i - 2:
                mm_out(i - 2)
            if live:
                recip(i, False)
                weigh(i, 0, LASTW[0] if last else "G")
                weigh(i, 1, LASTW[1] if last else "G")
            for h, c in inters[:NG]:
                v_inter(h, c, 0, 128, "G")
            for h, c in vqs:
                if (h, c) in by_g and NG > 1:
                    v_inter(h, c, 128, 256, "G")
            by_g.update(inters)
            if 0 <= i - 2 and OUT_FIRST:
                store(i - 2)
            if 0 <= i + 1 < UNITS:
                neg_scale(i + 1)
                exps(i + 1)
            if 0 < i + 2 < UNITS:
                row_max(i + 2, 0)
                row_max(i + 2, 1)
            if 0 <= i - 2 and not OUT_FIRST:
                store(i - 2)
            for kind, item in others[:1]:
                piece(kind, item, None, 0)
            for n, (kind, item) in enumerate(jobs[:1]):
                piece(kind, item, "w1", PADP if i < 0 else PADJ)
            if prev:
                gain(i - 1, 0)
                if i == UNITS:
                    a_quant(i - 1, 0, 1)
                gain(i - 1, 1)
            for job in quants:
                job_quant(job)
            for h, c in vqs:
                v_quant(h, c)
            if 0 < i + 3 < UNITS:
                mm_scores(i + 3, PADS)
            for n, (kind, item) in enumerate(jobs[1:]):
                piece(kind, item, ("w0", "w1")[n % 2], PADP if i < 0 else 0)
            for kind, item in others[1:]:
                piece(kind, item, None, 0)
            if live:
                turn(i, 0, PADT if jobs or i < 10 else 0)
                turn(i, 1, PADU)
            if prev:
                if i == UNITS:
                    a_quant(i - 1, 1, 2)
                else:
                    a_quant(i - 1, 0, 2)
            for h, c in inters:
                if NG == 0:
                    v_inter(h, c, 0, 256, "V")
                if NG == 1:
                    v_inter(h, c, 128, 256, "V")
                v_inter(h, c, 256, 512, "V")
            quants, next_quants = next_quants, []
            vqs, next_vqs = list(inters) + next_vqs, []
            inters, next_inters = next_inters, []
        mm_out(UNITS - 1)
        store(UNITS - 1)
